import numpy as np
import ml_dtypes


def mxq(x, axis, fmt="e4m3"):
    dtype, down = {"e4m3": (ml_dtypes.float8_e4m3fn, 7), "e5m2": (ml_dtypes.float8_e5m2, 14)}[fmt]
    v = np.moveaxis(np.asarray(x, np.float32).astype(ml_dtypes.bfloat16).astype(np.float64), axis, -1)
    blocks = v.reshape(v.shape[:-1] + (-1, 32))
    amax = np.abs(blocks).max(-1, keepdims=True)
    byte = np.maximum(np.where(amax > 0, np.frexp(amax)[1] - 1 + 127, 0) - down, 1)
    scale = np.exp2(byte - 127.0)
    codes = (blocks / scale).astype(np.float32).astype(dtype).astype(np.float64)
    return np.moveaxis((codes * scale).reshape(v.shape), -1, axis)


WIDE = False


def mx_kscale(k):
    if not WIDE:
        return np.ones(k)
    levels = np.array([10, -10, 5, -5, 0])
    if k % 512:
        return np.exp2(np.random.permutation(np.resize(levels, k // 32))).repeat(32)
    a = np.empty((k // 512, 16))
    for p in range(k // 512):
        a[p, :8] = np.random.permutation(np.resize(levels, 8))
        for g in range(8):
            far = levels[np.abs(levels - a[p, g]) >= 10]
            a[p, g + 8] = far[np.random.randint(len(far))]
    return np.exp2(a.ravel()).repeat(32)


def f64(x):
    return np.asarray(x).astype(np.float64)


def striped(idx):
    return np.tile(np.asarray(idx).reshape(-1, 16).T, (8, 1)).astype(np.uint16)


def unstriped(offs):
    return offs[:16].T.reshape(-1).astype(np.int64)

def sigmoid(v):
    return 1.0 / (1.0 + np.exp(-v))


B, N, T, D, NQ = 1, 512, 2048, 512, 256


def setup_inputs():
    n = np.random.standard_normal
    idx = np.random.permutation(T)[:B * N]
    idx2 = np.random.permutation(1024)[:B * N]
    s = mx_kscale(D)[:, None]
    return {
        "qT": (n((B, D, NQ)) * s * (1.00 / np.sqrt(D))).astype(np.float32),
        "pT": (n((B, D, NQ)) * s * (1.00 / np.sqrt(D))).astype(np.float32),
        "kT": (np.clip(np.round(n((D, T)) * 16), -64, 64) / 16 / s).astype(np.float32),
        "rT": (np.clip(np.round(n((D, 1024)) * 16), -64, 64) / 16).astype(np.float32),
        "offs": striped(idx),
        "offs2": striped(idx2),
    }


def reference(qT, pT, kT, rT, offs, offs2):
    idx = unstriped(offs)
    idx2 = unstriped(offs2)
    pick = lambda x, which: x[:, which].reshape(x.shape[0], B, -1).transpose(1, 0, 2)
    kg = mxq(pick(f64(kT), idx), 1, "e4m3")
    rg = pick(f64(rT), idx2)
    ug = mxq(pick(f64(kT), idx) * rg, 1, "e4m3")
    qq = mxq(f64(qT), 1, "e4m3")
    pq = mxq(f64(pT), 1, "e4m3")
    a = (qq.transpose(0, 2, 1) @ ug) + (pq.transpose(0, 2, 1) @ kg)
    y = sigmoid(a)
    return y

@@ -1,0 +1,175 @@
+from contextlib import ExitStack
+
+import concourse.mybir as mybir
+
+F32 = mybir.dt.float32
+BF16 = mybir.dt.bfloat16
+U32 = mybir.dt.uint32
+U16 = mybir.dt.uint16
+U8 = mybir.dt.uint8
+FP8X4 = mybir.dt.float8_e4m3fn_x4
+MULT = mybir.AluOpType.mult
+SIGMOID = mybir.ActivationFunctionType.Sigmoid
+
+P = 128
+PACK = 4
+D = 512
+SLOTS = 512
+NQ = 256
+T_K = 2048
+T_R = 1024
+HALF = SLOTS // 2
+LIST_COLS = SLOTS // 16
+
+FLOPS = 2 * 2 * D * NQ * SLOTS
+
+
+def tile_attend_pre_din_f_topk_kernel(tc, qT, pT, kT, rT, offs, offs2, out):
+    nc = tc.nc
+    with ExitStack() as ctx:
+        lists = ctx.enter_context(tc.tile_pool(name="lists", bufs=1))
+        sb = ctx.enter_context(tc.tile_pool(name="sb", bufs=1))
+        psum = ctx.enter_context(tc.psum_pool(name="psum", bufs=1))
+
+        k_list = lists.tile([P, LIST_COLS], U16, name="k_list")
+        r_list = lists.tile([P, LIST_COLS], U16, name="r_list")
+        k_plane = [sb.tile([P, T_K], F32, name=f"k_plane{t}") for t in range(PACK)]
+        r_plane = [sb.tile([P, T_R], F32, name=f"r_plane{t}") for t in range(PACK)]
+        p_raw = sb.tile([P, PACK, NQ], F32, name="p_raw", tag="p_raw", align_bytes=64)
+        q_raw = sb.tile([P, PACK, NQ], F32, name="q_raw")
+
+        k_rows = kT.rearrange("(p t) w -> p t w", t=PACK)
+        r_rows = rT.rearrange("(p t) w -> p t w", t=PACK)
+
+        warm_in = sb.tile([P, 1], F32, name="warm_in")
+        warm_out = sb.tile([P, 1], F32, name="warm_out")
+        nc.vector.memset(warm_in[:], 0.0)
+        nc.scalar.activation(warm_out[:], warm_in[:], SIGMOID)
+
+        nc.sync.dma_start(k_plane[0][:], k_rows[:, 0, :])
+        nc.sync.dma_start(k_list[:], offs)
+        nc.sync.dma_start(r_list[:], offs2)
+        nc.sync.dma_start(r_plane[0][:], r_rows[:, 0, :])
+        nc.sync.dma_start(k_plane[1][:], k_rows[:, 1, :])
+        nc.sync.dma_start(r_plane[1][:], r_rows[:, 1, :])
+        nc.sync.dma_start(k_plane[2][:], k_rows[:, 2, :])
+        nc.sync.dma_start(k_plane[3][:], k_rows[:, 3, :])
+        nc.sync.dma_start(r_plane[2][:], r_rows[:, 2, :])
+        nc.sync.dma_start(r_plane[3][:], r_rows[:, 3, :])
+        nc.sync.dma_start(p_raw[:], pT[0].rearrange("(p t) w -> p t w", t=PACK))
+        nc.sync.dma_start(q_raw[:], qT[0].rearrange("(p t) w -> p t w", t=PACK))
+
+        k_pair = [sb.tile([P, 2, SLOTS], F32, name=f"k_pair{j}", tag=f"k_pair{j}", align_bytes=64) for j in range(2)]
+        u_pair = [sb.tile([P, 2, SLOTS], F32, name=f"u_pair{j}") for j in range(2)]
+
+        def tiles(name, shape, dtype):
+            return [sb.tile(shape, dtype, name=f"{name}{h}", tag=f"{name}{h}", align_bytes=64) for h in range(2)]
+
+        k_bf, u_bf = tiles("k_bf", [P, HALF, PACK], BF16), tiles("u_bf", [P, HALF, PACK], BF16)
+        p_bf, q_bf = tiles("p_bf", [P, P, PACK], BF16), tiles("q_bf", [P, P, PACK], BF16)
+        k_codes, u_codes = {}, {}
+
+        def codes_on(tag, name):
+            return sb.tile([P, HALF], U32, name=name, tag=tag, align_bytes=64)
+
+        k_scales, u_scales = tiles("k_scales", [P, HALF], U8), tiles("u_scales", [P, HALF], U8)
+        p_codes, q_codes = tiles("p_codes", [P, P], U32), tiles("q_codes", [P, P], U32)
+        p_scales, q_scales = tiles("p_scales", [P, P], U8), tiles("q_scales", [P, P], U8)
+
+        def gather_k(t, lo, hi):
+            nc.vector.tensor_copy(
+                k_pair[t // 2][:, t % 2, lo:hi], k_plane[t][:].indirect(k_list[:, lo // 16 : hi // 16])
+            )
+
+        def gather_r(t, lo, hi):
+            nc.vector.tensor_tensor(
+                u_pair[t // 2][:, t % 2, lo:hi],
+                r_plane[t][:].indirect(r_list[:, lo // 16 : hi // 16]),
+                k_pair[t // 2][:, t % 2, lo:hi],
+                MULT,
+            )
+
+        def copy_on(engine, dst, src):
+            if engine == "scalar":
+                nc.scalar.copy(dst, src)
+            else:
+                nc.vector.tensor_copy(dst, src)
+
+        def lay_pair(engine, dst, src, j, h):
+            copy_on(
+                engine,
+                dst[h][:, :, 2 * j : 2 * j + 2],
+                src[j][:, :, h * HALF : (h + 1) * HALF].rearrange("p e n -> p n e"),
+            )
+
+        def lay_weights(engine, dst, raw, m):
+            copy_on(
+                engine,
+                dst[m][:].rearrange("p (c i) t -> p c t i", i=4),
+                raw[:, :, m * P : (m + 1) * P].rearrange("p t (c i) -> p c t i", i=4),
+            )
+
+        def quantize(codes, scales, src):
+            nc.vector.quantize_mx(
+                out=codes[:].bitcast(FP8X4), scales=scales[:], in_=src[:].rearrange("p n t -> p (n t)")
+            )
+
+        acc = {(m, h): psum.tile([P, HALF], F32, name=f"acc{m}{h}") for m in range(2) for h in range(2)}
+
+        def product(m, h, w_codes, w_scales, x_codes, x_scales, first):
+            nc.tensor.matmul_mx(
+                out=acc[m, h][:],
+                lhsT=w_codes[m][:].bitcast(FP8X4),
+                lhsT_scale=w_scales[m][:],
+                rhs=x_codes[h][:].bitcast(FP8X4),
+                rhs_scale=x_scales[h][:],
+                start=first,
+                stop=not first,
+            )
+
+        def finish(m, h):
+            product(m, h, q_codes, q_scales, u_codes, u_scales, False)
+            res = sb.tile([P, HALF], F32, name=f"res{m}{h}")
+            nc.scalar.activation(res[:], acc[m, h][:], SIGMOID)
+            nc.sync.dma_start(out[0, m * P : (m + 1) * P, h * HALF : (h + 1) * HALF], res[:])
+
+        gather_k(0, 0, SLOTS)
+        gather_r(0, 0, SLOTS)
+        gather_k(1, 0, SLOTS)
+        for h in range(2):
+            lay_pair("scalar", k_bf, k_pair, 0, h)
+        gather_r(1, 0, SLOTS)
+        for h in range(2):
+            lay_pair("scalar", u_bf, u_pair, 0, h)
+        gather_k(2, 0, SLOTS)
+        gather_k(3, 0, SLOTS)
+        for h in range(2):
+            lay_pair("scalar", k_bf, k_pair, 1, h)
+        gather_r(2, 0, SLOTS)
+        gather_r(3, 0, HALF)
+        gather_r(3, HALF, SLOTS)
+        for h in range(2):
+            lay_pair("vector", u_bf, u_pair, 1, h)
+        k_codes[0] = codes_on("k_pair1", "k_codes0")
+        quantize(k_codes[0], k_scales[0], k_bf[0])
+        for m in range(2):
+            lay_weights("scalar", p_bf, p_raw, m)
+        for m in range(2):
+            quantize(p_codes[m], p_scales[m], p_bf[m])
+            product(m, 0, p_codes, p_scales, k_codes, k_scales, True)
+        k_codes[1] = codes_on("p_raw", "k_codes1")
+        quantize(k_codes[1], k_scales[1], k_bf[1])
+        for m in range(2):
+            product(m, 1, p_codes, p_scales, k_codes, k_scales, True)
+        for m in range(2):
+            lay_weights("scalar", q_bf, q_raw, m)
+        u_codes[0] = codes_on("p_bf1", "u_codes0")
+        quantize(u_codes[0], u_scales[0], u_bf[0])
+        quantize(q_codes[0], q_scales[0], q_bf[0])
+        finish(0, 0)
+        u_codes[1] = codes_on("k_bf1", "u_codes1")
+        quantize(u_codes[1], u_scales[1], u_bf[1])
+        finish(0, 1)
+        quantize(q_codes[1], q_scales[1], q_bf[1])
+        finish(1, 0)
+        finish(1, 1)

@@ -41,23 +41,23 @@ def tile_attend_pre_din_f_topk_kernel(tc, qT, pT, kT, rT, offs, offs2, out):
         k_rows = kT.rearrange("(p t) w -> p t w", t=PACK)
         r_rows = rT.rearrange("(p t) w -> p t w", t=PACK)
 
-        warm_in = sb.tile([P, 1], F32, name="warm_in")
-        warm_out = sb.tile([P, 1], F32, name="warm_out")
-        nc.vector.memset(warm_in[:], 0.0)
-        nc.scalar.activation(warm_out[:], warm_in[:], SIGMOID)
-
-        nc.sync.dma_start(k_plane[0][:], k_rows[:, 0, :])
+        nc.scalar.dma_start(k_plane[0][:], k_rows[:, 0, :])
         nc.sync.dma_start(k_list[:], offs)
         nc.sync.dma_start(r_list[:], offs2)
         nc.sync.dma_start(r_plane[0][:], r_rows[:, 0, :])
         nc.sync.dma_start(k_plane[1][:], k_rows[:, 1, :])
-        nc.sync.dma_start(r_plane[1][:], r_rows[:, 1, :])
+        nc.scalar.dma_start(r_plane[1][:], r_rows[:, 1, :])
         nc.sync.dma_start(k_plane[2][:], k_rows[:, 2, :])
         nc.sync.dma_start(k_plane[3][:], k_rows[:, 3, :])
         nc.sync.dma_start(r_plane[2][:], r_rows[:, 2, :])
         nc.sync.dma_start(r_plane[3][:], r_rows[:, 3, :])
         nc.sync.dma_start(p_raw[:], pT[0].rearrange("(p t) w -> p t w", t=PACK))
         nc.sync.dma_start(q_raw[:], qT[0].rearrange("(p t) w -> p t w", t=PACK))
+
+        warm_in = sb.tile([P, 1], F32, name="warm_in")
+        warm_out = sb.tile([P, 1], F32, name="warm_out")
+        nc.vector.memset(warm_in[:], 0.0)
+        nc.scalar.activation(warm_out[:], warm_in[:], SIGMOID)
 
         k_pair = [sb.tile([P, 2, SLOTS], F32, name=f"k_pair{j}", tag=f"k_pair{j}", align_bytes=64) for j in range(2)]
         u_pair = [sb.tile([P, 2, SLOTS], F32, name=f"u_pair{j}") for j in range(2)]

@@ -10,6 +10,7 @@ U8 = mybir.dt.uint8
 FP8X4 = mybir.dt.float8_e4m3fn_x4
 MULT = mybir.AluOpType.mult
 SIGMOID = mybir.ActivationFunctionType.Sigmoid
+COPY = mybir.ActivationFunctionType.Copy
 
 P = 128
 PACK = 4
@@ -19,7 +20,10 @@ NQ = 256
 T_K = 2048
 T_R = 1024
 HALF = SLOTS // 2
+QUARTER = SLOTS // 4
 LIST_COLS = SLOTS // 16
+FUSED = 128
+R3_CUTS = (FUSED, 192, 352, SLOTS)
 
 FLOPS = 2 * 2 * D * NQ * SLOTS
 
@@ -44,9 +48,9 @@ def tile_attend_pre_din_f_topk_kernel(tc, qT, pT, kT, rT, offs, offs2, out):
         nc.scalar.dma_start(k_plane[0][:], k_rows[:, 0, :])
         nc.sync.dma_start(k_list[:], offs)
         nc.sync.dma_start(r_list[:], offs2)
-        nc.sync.dma_start(r_plane[0][:], r_rows[:, 0, :])
         nc.sync.dma_start(k_plane[1][:], k_rows[:, 1, :])
-        nc.scalar.dma_start(r_plane[1][:], r_rows[:, 1, :])
+        nc.sync.dma_start(r_plane[0][:], r_rows[:, 0, :])
+        nc.sync.dma_start(r_plane[1][:], r_rows[:, 1, :])
         nc.sync.dma_start(k_plane[2][:], k_rows[:, 2, :])
         nc.sync.dma_start(k_plane[3][:], k_rows[:, 3, :])
         nc.sync.dma_start(r_plane[2][:], r_rows[:, 2, :])
@@ -59,34 +63,38 @@ def tile_attend_pre_din_f_topk_kernel(tc, qT, pT, kT, rT, offs, offs2, out):
         nc.vector.memset(warm_in[:], 0.0)
         nc.scalar.activation(warm_out[:], warm_in[:], SIGMOID)
 
-        k_pair = [sb.tile([P, 2, SLOTS], F32, name=f"k_pair{j}", tag=f"k_pair{j}", align_bytes=64) for j in range(2)]
-        u_pair = [sb.tile([P, 2, SLOTS], F32, name=f"u_pair{j}") for j in range(2)]
+        k_pair = [sb.tile([P, 2, SLOTS], F32, name=f"k_pair{j}") for j in range(2)]
+        u_early = sb.tile([P, 2, SLOTS], F32, name="u_early")
+        u_late = sb.tile([P, 2, FUSED], F32, name="u_late")
+        r_late = sb.tile([P, 2, SLOTS - FUSED], F32, name="r_late")
 
-        def tiles(name, shape, dtype):
-            return [sb.tile(shape, dtype, name=f"{name}{h}", tag=f"{name}{h}", align_bytes=64) for h in range(2)]
+        def mx_tile(name, shape, dtype, tag=None):
+            return sb.tile(shape, dtype, name=name, tag=tag or name, align_bytes=64)
 
-        k_bf, u_bf = tiles("k_bf", [P, HALF, PACK], BF16), tiles("u_bf", [P, HALF, PACK], BF16)
-        p_bf, q_bf = tiles("p_bf", [P, P, PACK], BF16), tiles("q_bf", [P, P, PACK], BF16)
+        k_bf, u_bf = mx_tile("k_bf", [P, SLOTS, PACK], BF16), mx_tile("u_bf", [P, SLOTS, PACK], BF16)
+        p_bf = [mx_tile(f"p_bf{m}", [P, P, PACK], BF16) for m in range(2)]
+        q_bf = [mx_tile(f"q_bf{m}", [P, P, PACK], BF16) for m in range(2)]
+        k_scales = [mx_tile(f"k_scales{h}", [P, HALF], U8) for h in range(2)]
+        u_scales = [mx_tile(f"u_scales{h}", [P, HALF], U8) for h in range(2)]
+        p_scales = [mx_tile(f"p_scales{m}", [P, P], U8) for m in range(2)]
+        q_scales = [mx_tile(f"q_scales{m}", [P, P], U8) for m in range(2)]
+        p_codes = [mx_tile(f"p_codes{m}", [P, P], U32) for m in range(2)]
+        q_codes = [mx_tile(f"q_codes{m}", [P, P], U32) for m in range(2)]
         k_codes, u_codes = {}, {}
 
-        def codes_on(tag, name):
-            return sb.tile([P, HALF], U32, name=name, tag=tag, align_bytes=64)
+        def gather(engine, dst, plane, offsets, lo, hi):
+            picked = plane[:].indirect(offsets[:, lo // 16 : hi // 16])
+            if engine == "scalar":
+                nc.scalar.activation(dst, picked, COPY)
+            else:
+                nc.vector.tensor_copy(dst, picked)
 
-        k_scales, u_scales = tiles("k_scales", [P, HALF], U8), tiles("u_scales", [P, HALF], U8)
-        p_codes, q_codes = tiles("p_codes", [P, P], U32), tiles("q_codes", [P, P], U32)
-        p_scales, q_scales = tiles("p_scales", [P, P], U8), tiles("q_scales", [P, P], U8)
+        def gather_k(engine, t, lo, hi):
+            gather(engine, k_pair[t // 2][:, t % 2, lo:hi], k_plane[t], k_list, lo, hi)
 
-        def gather_k(t, lo, hi):
-            nc.vector.tensor_copy(
-                k_pair[t // 2][:, t % 2, lo:hi], k_plane[t][:].indirect(k_list[:, lo // 16 : hi // 16])
-            )
-
-        def gather_r(t, lo, hi):
+        def gather_times_k(dst, t, hi):
             nc.vector.tensor_tensor(
-                u_pair[t // 2][:, t % 2, lo:hi],
-                r_plane[t][:].indirect(r_list[:, lo // 16 : hi // 16]),
-                k_pair[t // 2][:, t % 2, lo:hi],
-                MULT,
+                dst[:, t % 2, :], r_plane[t][:].indirect(r_list[:, : hi // 16]), k_pair[t // 2][:, t % 2, :hi], MULT
             )
 
         def copy_on(engine, dst, src):
@@ -95,11 +103,15 @@ def tile_attend_pre_din_f_topk_kernel(tc, qT, pT, kT, rT, offs, offs2, out):
             else:
                 nc.vector.tensor_copy(dst, src)
 
-        def lay_pair(engine, dst, src, j, h):
-            copy_on(
-                engine,
-                dst[h][:, :, 2 * j : 2 * j + 2],
-                src[j][:, :, h * HALF : (h + 1) * HALF].rearrange("p e n -> p n e"),
+        def by_slot(pair, lo, hi):
+            return pair[:, :, lo:hi].rearrange("p e n -> p n e")
+
+        def lay_pair(engine, dst, src, j, lo, hi):
+            copy_on(engine, dst[:, lo:hi, 2 * j : 2 * j + 2], by_slot(src, lo, hi))
+
+        def multiply_and_lay(lo, hi):
+            nc.vector.tensor_tensor(
+                u_bf[:, lo:hi, 2:4], by_slot(r_late, lo - FUSED, hi - FUSED), by_slot(k_pair[1], lo, hi), MULT
             )
 
         def lay_weights(engine, dst, raw, m):
@@ -110,9 +122,11 @@ def tile_attend_pre_din_f_topk_kernel(tc, qT, pT, kT, rT, offs, offs2, out):
             )
 
         def quantize(codes, scales, src):
-            nc.vector.quantize_mx(
-                out=codes[:].bitcast(FP8X4), scales=scales[:], in_=src[:].rearrange("p n t -> p (n t)")
-            )
+            nc.vector.quantize_mx(out=codes[:].bitcast(FP8X4), scales=scales[:], in_=src.rearrange("p n t -> p (n t)"))
+
+        def quantize_slots(codes, scales, src, h, name, tag=None):
+            codes[h] = mx_tile(name, [P, HALF], U32, tag=tag)
+            quantize(codes[h], scales[h], src[:, h * HALF : (h + 1) * HALF, :])
 
         acc = {(m, h): psum.tile([P, HALF], F32, name=f"acc{m}{h}") for m in range(2) for h in range(2)}
 
@@ -127,49 +141,56 @@ def tile_attend_pre_din_f_topk_kernel(tc, qT, pT, kT, rT, offs, offs2, out):
                 stop=not first,
             )
 
+        gather_k("vector", 0, 0, SLOTS)
+        gather_k("vector", 1, 0, SLOTS)
+        lay_pair("scalar", k_bf, k_pair[0], 0, 0, SLOTS)
+        gather_times_k(u_early, 0, SLOTS)
+        gather_times_k(u_early, 1, SLOTS)
+        lay_pair("scalar", u_bf, u_early, 0, 0, SLOTS)
+        gather_k("vector", 2, 0, SLOTS)
+
+        gather_k("vector", 3, 0, QUARTER)
+        for c in range(1, 4):
+            gather_k("scalar", 3, c * QUARTER, (c + 1) * QUARTER)
+        lay_pair("vector", k_bf, k_pair[1], 1, 0, HALF)
+        lay_pair("vector", k_bf, k_pair[1], 1, HALF, HALF + QUARTER)
+        lay_pair("vector", k_bf, k_pair[1], 1, HALF + QUARTER, SLOTS)
+        quantize_slots(k_codes, k_scales, k_bf, 0, "k_codes0")
+
+        gather("scalar", r_late[:, 0, :], r_plane[2], r_list, FUSED, SLOTS)
+        gather_times_k(u_late, 2, FUSED)
+        gather_times_k(u_late, 3, FUSED)
+        pieces = list(zip(R3_CUTS[:-1], R3_CUTS[1:]))
+        for lo, hi in pieces:
+            gather("scalar", r_late[:, 1, lo - FUSED : hi - FUSED], r_plane[3], r_list, lo, hi)
+        multiply_and_lay(*pieces[0])
+        lay_pair("vector", u_bf, u_late, 1, 0, FUSED)
+        for lo, hi in pieces[1:]:
+            multiply_and_lay(lo, hi)
+
+        for m in range(2):
+            lay_weights("scalar", p_bf, p_raw, m)
+        quantize(p_codes[0], p_scales[0], p_bf[0][:])
+        product(0, 0, p_codes, p_scales, k_codes, k_scales, True)
+        quantize_slots(k_codes, k_scales, k_bf, 1, "k_codes1", tag="p_bf0")
+        product(0, 1, p_codes, p_scales, k_codes, k_scales, True)
+        quantize(p_codes[1], p_scales[1], p_bf[1][:])
+        for h in range(2):
+            product(1, h, p_codes, p_scales, k_codes, k_scales, True)
+
         def finish(m, h):
             product(m, h, q_codes, q_scales, u_codes, u_scales, False)
             res = sb.tile([P, HALF], F32, name=f"res{m}{h}")
             nc.scalar.activation(res[:], acc[m, h][:], SIGMOID)
             nc.sync.dma_start(out[0, m * P : (m + 1) * P, h * HALF : (h + 1) * HALF], res[:])
 
-        gather_k(0, 0, SLOTS)
-        gather_r(0, 0, SLOTS)
-        gather_k(1, 0, SLOTS)
-        for h in range(2):
-            lay_pair("scalar", k_bf, k_pair, 0, h)
-        gather_r(1, 0, SLOTS)
-        for h in range(2):
-            lay_pair("scalar", u_bf, u_pair, 0, h)
-        gather_k(2, 0, SLOTS)
-        gather_k(3, 0, SLOTS)
-        for h in range(2):
-            lay_pair("scalar", k_bf, k_pair, 1, h)
-        gather_r(2, 0, SLOTS)
-        gather_r(3, 0, HALF)
-        gather_r(3, HALF, SLOTS)
-        for h in range(2):
-            lay_pair("vector", u_bf, u_pair, 1, h)
-        k_codes[0] = codes_on("k_pair1", "k_codes0")
-        quantize(k_codes[0], k_scales[0], k_bf[0])
-        for m in range(2):
-            lay_weights("scalar", p_bf, p_raw, m)
-        for m in range(2):
-            quantize(p_codes[m], p_scales[m], p_bf[m])
-            product(m, 0, p_codes, p_scales, k_codes, k_scales, True)
-        k_codes[1] = codes_on("p_raw", "k_codes1")
-        quantize(k_codes[1], k_scales[1], k_bf[1])
-        for m in range(2):
-            product(m, 1, p_codes, p_scales, k_codes, k_scales, True)
+        quantize_slots(u_codes, u_scales, u_bf, 0, "u_codes0", tag="p_raw")
         for m in range(2):
             lay_weights("scalar", q_bf, q_raw, m)
-        u_codes[0] = codes_on("p_bf1", "u_codes0")
-        quantize(u_codes[0], u_scales[0], u_bf[0])
-        quantize(q_codes[0], q_scales[0], q_bf[0])
+        quantize(q_codes[0], q_scales[0], q_bf[0][:])
         finish(0, 0)
-        u_codes[1] = codes_on("k_bf1", "u_codes1")
-        quantize(u_codes[1], u_scales[1], u_bf[1])
+        quantize_slots(u_codes, u_scales, u_bf, 1, "u_codes1", tag="q_bf0")
         finish(0, 1)
-        quantize(q_codes[1], q_scales[1], q_bf[1])
+        quantize(q_codes[1], q_scales[1], q_bf[1][:])
         finish(1, 0)
         finish(1, 1)

@@ -37,24 +37,24 @@ def tile_attend_pre_din_f_topk_kernel(tc, qT, pT, kT, rT, offs, offs2, out):
 
         k_list = lists.tile([P, LIST_COLS], U16, name="k_list")
         r_list = lists.tile([P, LIST_COLS], U16, name="r_list")
-        k_plane = [sb.tile([P, T_K], F32, name=f"k_plane{t}") for t in range(PACK)]
-        r_plane = [sb.tile([P, T_R], F32, name=f"r_plane{t}") for t in range(PACK)]
+        k_early = sb.tile([P, 2, T_K], F32, name="k_early")
+        r_early = sb.tile([P, 2, T_R], F32, name="r_early")
+        k_plane = [k_early[:, 0, :], k_early[:, 1, :]] + [sb.tile([P, T_K], F32, name=f"k_plane{t}")[:, :] for t in (2, 3)]
+        r_plane = [r_early[:, 0, :], r_early[:, 1, :]] + [sb.tile([P, T_R], F32, name=f"r_plane{t}")[:, :] for t in (2, 3)]
         p_raw = sb.tile([P, PACK, NQ], F32, name="p_raw", tag="p_raw", align_bytes=64)
         q_raw = sb.tile([P, PACK, NQ], F32, name="q_raw")
 
         k_rows = kT.rearrange("(p t) w -> p t w", t=PACK)
         r_rows = rT.rearrange("(p t) w -> p t w", t=PACK)
 
-        nc.scalar.dma_start(k_plane[0][:], k_rows[:, 0, :])
+        nc.sync.dma_start(k_early[:], k_rows[:, 0:2, :])
         nc.sync.dma_start(k_list[:], offs)
         nc.sync.dma_start(r_list[:], offs2)
-        nc.sync.dma_start(k_plane[1][:], k_rows[:, 1, :])
-        nc.sync.dma_start(r_plane[0][:], r_rows[:, 0, :])
-        nc.sync.dma_start(r_plane[1][:], r_rows[:, 1, :])
-        nc.sync.dma_start(k_plane[2][:], k_rows[:, 2, :])
-        nc.sync.dma_start(k_plane[3][:], k_rows[:, 3, :])
-        nc.sync.dma_start(r_plane[2][:], r_rows[:, 2, :])
-        nc.sync.dma_start(r_plane[3][:], r_rows[:, 3, :])
+        nc.sync.dma_start(r_early[:], r_rows[:, 0:2, :])
+        nc.sync.dma_start(k_plane[2], k_rows[:, 2, :])
+        nc.sync.dma_start(k_plane[3], k_rows[:, 3, :])
+        nc.sync.dma_start(r_plane[2], r_rows[:, 2, :])
+        nc.sync.dma_start(r_plane[3], r_rows[:, 3, :])
         nc.sync.dma_start(p_raw[:], pT[0].rearrange("(p t) w -> p t w", t=PACK))
         nc.sync.dma_start(q_raw[:], qT[0].rearrange("(p t) w -> p t w", t=PACK))
 
@@ -64,7 +64,7 @@ def tile_attend_pre_din_f_topk_kernel(tc, qT, pT, kT, rT, offs, offs2, out):
         nc.scalar.activation(warm_out[:], warm_in[:], SIGMOID)
 
         k_pair = [sb.tile([P, 2, SLOTS], F32, name=f"k_pair{j}") for j in range(2)]
-        u_early = sb.tile([P, 2, SLOTS], F32, name="u_early")
+        r_first = sb.tile([P, 2, SLOTS], F32, name="r_first")
         u_late = sb.tile([P, 2, FUSED], F32, name="u_late")
         r_late = sb.tile([P, 2, SLOTS - FUSED], F32, name="r_late")
 
@@ -83,7 +83,7 @@ def tile_attend_pre_din_f_topk_kernel(tc, qT, pT, kT, rT, offs, offs2, out):
         k_codes, u_codes = {}, {}
 
         def gather(engine, dst, plane, offsets, lo, hi):
-            picked = plane[:].indirect(offsets[:, lo // 16 : hi // 16])
+            picked = plane.indirect(offsets[:, lo // 16 : hi // 16])
             if engine == "scalar":
                 nc.scalar.activation(dst, picked, COPY)
             else:
@@ -94,7 +94,7 @@ def tile_attend_pre_din_f_topk_kernel(tc, qT, pT, kT, rT, offs, offs2, out):
 
         def gather_times_k(dst, t, hi):
             nc.vector.tensor_tensor(
-                dst[:, t % 2, :], r_plane[t][:].indirect(r_list[:, : hi // 16]), k_pair[t // 2][:, t % 2, :hi], MULT
+                dst[:, t % 2, :], r_plane[t].indirect(r_list[:, : hi // 16]), k_pair[t // 2][:, t % 2, :hi], MULT
             )
 
         def copy_on(engine, dst, src):
@@ -142,12 +142,12 @@ def tile_attend_pre_din_f_topk_kernel(tc, qT, pT, kT, rT, offs, offs2, out):
             )
 
         gather_k("vector", 0, 0, SLOTS)
-        gather_k("vector", 1, 0, SLOTS)
-        lay_pair("scalar", k_bf, k_pair[0], 0, 0, SLOTS)
-        gather_times_k(u_early, 0, SLOTS)
-        gather_times_k(u_early, 1, SLOTS)
-        lay_pair("scalar", u_bf, u_early, 0, 0, SLOTS)
-        gather_k("vector", 2, 0, SLOTS)
+        gather_k("scalar", 1, 0, SLOTS)
+        lay_pair("vector", k_bf, k_pair[0], 0, 0, SLOTS)
+        gather("vector", r_first[:, 0, :], r_plane[0], r_list, 0, SLOTS)
+        gather("scalar", r_first[:, 1, :], r_plane[1], r_list, 0, SLOTS)
+        nc.vector.tensor_tensor(u_bf[:, :, 0:2], by_slot(r_first, 0, SLOTS), by_slot(k_pair[0], 0, SLOTS), MULT)
+        gather_k("scalar", 2, 0, SLOTS)
 
         gather_k("vector", 3, 0, QUARTER)
         for c in range(1, 4):

@@ -22,6 +22,7 @@ T_R = 1024
 HALF = SLOTS // 2
 QUARTER = SLOTS // 4
 LIST_COLS = SLOTS // 16
+DMA_ALIGN = 256
 FUSED = 128
 R3_CUTS = (FUSED, 192, 352, SLOTS)
 
@@ -37,12 +38,14 @@ def tile_attend_pre_din_f_topk_kernel(tc, qT, pT, kT, rT, offs, offs2, out):
 
         k_list = lists.tile([P, LIST_COLS], U16, name="k_list")
         r_list = lists.tile([P, LIST_COLS], U16, name="r_list")
-        k_early = sb.tile([P, 2, T_K], F32, name="k_early")
-        r_early = sb.tile([P, 2, T_R], F32, name="r_early")
-        k_plane = [k_early[:, 0, :], k_early[:, 1, :]] + [sb.tile([P, T_K], F32, name=f"k_plane{t}")[:, :] for t in (2, 3)]
-        r_plane = [r_early[:, 0, :], r_early[:, 1, :]] + [sb.tile([P, T_R], F32, name=f"r_plane{t}")[:, :] for t in (2, 3)]
-        p_raw = sb.tile([P, PACK, NQ], F32, name="p_raw", tag="p_raw", align_bytes=64)
-        q_raw = sb.tile([P, PACK, NQ], F32, name="q_raw")
+        k_early = sb.tile([P, 2, T_K], F32, name="k_early", align_bytes=DMA_ALIGN)
+        r_early = sb.tile([P, 2, T_R], F32, name="r_early", align_bytes=DMA_ALIGN)
+        k_late = [sb.tile([P, T_K], F32, name=f"k_plane{t}", align_bytes=DMA_ALIGN) for t in (2, 3)]
+        r_late_planes = [sb.tile([P, T_R], F32, name=f"r_plane{t}", align_bytes=DMA_ALIGN) for t in (2, 3)]
+        k_plane = [k_early[:, 0, :], k_early[:, 1, :], k_late[0][:], k_late[1][:]]
+        r_plane = [r_early[:, 0, :], r_early[:, 1, :], r_late_planes[0][:], r_late_planes[1][:]]
+        p_raw = sb.tile([P, PACK, NQ], F32, name="p_raw", tag="p_raw", align_bytes=DMA_ALIGN)
+        q_raw = sb.tile([P, PACK, NQ], F32, name="q_raw", align_bytes=DMA_ALIGN)
 
         k_rows = kT.rearrange("(p t) w -> p t w", t=PACK)
         r_rows = rT.rearrange("(p t) w -> p t w", t=PACK)
@@ -69,7 +72,7 @@ def tile_attend_pre_din_f_topk_kernel(tc, qT, pT, kT, rT, offs, offs2, out):
         r_late = sb.tile([P, 2, SLOTS - FUSED], F32, name="r_late")
 
         def mx_tile(name, shape, dtype, tag=None):
-            return sb.tile(shape, dtype, name=name, tag=tag or name, align_bytes=64)
+            return sb.tile(shape, dtype, name=name, tag=tag or name, align_bytes=DMA_ALIGN if tag == "p_raw" else 64)
 
         k_bf, u_bf = mx_tile("k_bf", [P, SLOTS, PACK], BF16), mx_tile("u_bf", [P, SLOTS, PACK], BF16)
         p_bf = [mx_tile(f"p_bf{m}", [P, P, PACK], BF16) for m in range(2)]
@@ -180,7 +183,7 @@ def tile_attend_pre_din_f_topk_kernel(tc, qT, pT, kT, rT, offs, offs2, out):
 
         def finish(m, h):
             product(m, h, q_codes, q_scales, u_codes, u_scales, False)
-            res = sb.tile([P, HALF], F32, name=f"res{m}{h}")
+            res = sb.tile([P, HALF], F32, name=f"res{m}{h}", align_bytes=DMA_ALIGN)
             nc.scalar.activation(res[:], acc[m, h][:], SIGMOID)
             nc.sync.dma_start(out[0, m * P : (m + 1) * P, h * HALF : (h + 1) * HALF], res[:])
 

@@ -23,8 +23,8 @@ HALF = SLOTS // 2
 QUARTER = SLOTS // 4
 LIST_COLS = SLOTS // 16
 DMA_ALIGN = 256
-FUSED = 128
-R3_CUTS = (FUSED, 192, 352, SLOTS)
+FUSED = 96
+R3_CUTS = (FUSED, 160, 352, SLOTS)
 
 FLOPS = 2 * 2 * D * NQ * SLOTS
 
@@ -158,7 +158,8 @@ def tile_attend_pre_din_f_topk_kernel(tc, qT, pT, kT, rT, offs, offs2, out):
         lay_pair("vector", k_bf, k_pair[1], 1, 0, HALF)
         lay_pair("vector", k_bf, k_pair[1], 1, HALF, HALF + QUARTER)
         lay_pair("vector", k_bf, k_pair[1], 1, HALF + QUARTER, SLOTS)
-        quantize_slots(k_codes, k_scales, k_bf, 0, "k_codes0")
+        for h in range(2):
+            quantize_slots(k_codes, k_scales, k_bf, h, f"k_codes{h}")
 
         gather("scalar", r_late[:, 0, :], r_plane[2], r_list, FUSED, SLOTS)
         gather_times_k(u_late, 2, FUSED)
@@ -174,9 +175,9 @@ def tile_attend_pre_din_f_topk_kernel(tc, qT, pT, kT, rT, offs, offs2, out):
         for m in range(2):
             lay_weights("scalar", p_bf, p_raw, m)
         quantize(p_codes[0], p_scales[0], p_bf[0][:])
-        product(0, 0, p_codes, p_scales, k_codes, k_scales, True)
-        quantize_slots(k_codes, k_scales, k_bf, 1, "k_codes1", tag="p_bf0")
-        product(0, 1, p_codes, p_scales, k_codes, k_scales, True)
+        for h in range(2):
+            product(0, h, p_codes, p_scales, k_codes, k_scales, True)
+        quantize_slots(u_codes, u_scales, u_bf, 0, "u_codes0", tag="p_bf0")
         quantize(p_codes[1], p_scales[1], p_bf[1][:])
         for h in range(2):
             product(1, h, p_codes, p_scales, k_codes, k_scales, True)
@@ -187,12 +188,11 @@ def tile_attend_pre_din_f_topk_kernel(tc, qT, pT, kT, rT, offs, offs2, out):
             nc.scalar.activation(res[:], acc[m, h][:], SIGMOID)
             nc.sync.dma_start(out[0, m * P : (m + 1) * P, h * HALF : (h + 1) * HALF], res[:])
 
-        quantize_slots(u_codes, u_scales, u_bf, 0, "u_codes0", tag="p_raw")
+        quantize_slots(u_codes, u_scales, u_bf, 1, "u_codes1", tag="p_raw")
         for m in range(2):
             lay_weights("scalar", q_bf, q_raw, m)
         quantize(q_codes[0], q_scales[0], q_bf[0][:])
         finish(0, 0)
-        quantize_slots(u_codes, u_scales, u_bf, 1, "u_codes1", tag="q_bf0")
         finish(0, 1)
         quantize(q_codes[1], q_scales[1], q_bf[1][:])
         finish(1, 0)

@@ -44,8 +44,8 @@ def tile_attend_pre_din_f_topk_kernel(tc, qT, pT, kT, rT, offs, offs2, out):
         r_late_planes = [sb.tile([P, T_R], F32, name=f"r_plane{t}", align_bytes=DMA_ALIGN) for t in (2, 3)]
         k_plane = [k_early[:, 0, :], k_early[:, 1, :], k_late[0][:], k_late[1][:]]
         r_plane = [r_early[:, 0, :], r_early[:, 1, :], r_late_planes[0][:], r_late_planes[1][:]]
-        p_raw = sb.tile([P, PACK, NQ], F32, name="p_raw", tag="p_raw", align_bytes=DMA_ALIGN)
-        q_raw = sb.tile([P, PACK, NQ], F32, name="q_raw", align_bytes=DMA_ALIGN)
+        p_raw = [sb.tile([P, PACK, P], F32, name=f"p_raw{m}", tag=f"p_raw{m}", align_bytes=DMA_ALIGN) for m in range(2)]
+        q_raw = [sb.tile([P, PACK, P], F32, name=f"q_raw{m}", tag=f"q_raw{m}", align_bytes=DMA_ALIGN) for m in range(2)]
 
         k_rows = kT.rearrange("(p t) w -> p t w", t=PACK)
         r_rows = rT.rearrange("(p t) w -> p t w", t=PACK)
@@ -58,8 +58,11 @@ def tile_attend_pre_din_f_topk_kernel(tc, qT, pT, kT, rT, offs, offs2, out):
         nc.sync.dma_start(k_plane[3], k_rows[:, 3, :])
         nc.sync.dma_start(r_plane[2], r_rows[:, 2, :])
         nc.sync.dma_start(r_plane[3], r_rows[:, 3, :])
-        nc.sync.dma_start(p_raw[:], pT[0].rearrange("(p t) w -> p t w", t=PACK))
-        nc.sync.dma_start(q_raw[:], qT[0].rearrange("(p t) w -> p t w", t=PACK))
+        p_rows = pT[0].rearrange("(p t) w -> p t w", t=PACK)
+        q_rows = qT[0].rearrange("(p t) w -> p t w", t=PACK)
+        for m in range(2):
+            nc.sync.dma_start(p_raw[m][:], p_rows[:, :, m * P : (m + 1) * P])
+            nc.sync.dma_start(q_raw[m][:], q_rows[:, :, m * P : (m + 1) * P])
 
         warm_in = sb.tile([P, 1], F32, name="warm_in")
         warm_out = sb.tile([P, 1], F32, name="warm_out")
@@ -72,7 +75,7 @@ def tile_attend_pre_din_f_topk_kernel(tc, qT, pT, kT, rT, offs, offs2, out):
         r_late = sb.tile([P, 2, SLOTS - FUSED], F32, name="r_late")
 
         def mx_tile(name, shape, dtype, tag=None):
-            return sb.tile(shape, dtype, name=name, tag=tag or name, align_bytes=DMA_ALIGN if tag == "p_raw" else 64)
+            return sb.tile(shape, dtype, name=name, tag=tag or name, align_bytes=DMA_ALIGN)
 
         k_bf, u_bf = mx_tile("k_bf", [P, SLOTS, PACK], BF16), mx_tile("u_bf", [P, SLOTS, PACK], BF16)
         p_bf = [mx_tile(f"p_bf{m}", [P, P, PACK], BF16) for m in range(2)]
@@ -121,7 +124,7 @@ def tile_attend_pre_din_f_topk_kernel(tc, qT, pT, kT, rT, offs, offs2, out):
             copy_on(
                 engine,
                 dst[m][:].rearrange("p (c i) t -> p c t i", i=4),
-                raw[:, :, m * P : (m + 1) * P].rearrange("p t (c i) -> p c t i", i=4),
+                raw[m][:].rearrange("p t (c i) -> p c t i", i=4),
             )
 
         def quantize(codes, scales, src):
@@ -174,13 +177,7 @@ def tile_attend_pre_din_f_topk_kernel(tc, qT, pT, kT, rT, offs, offs2, out):
 
         for m in range(2):
             lay_weights("scalar", p_bf, p_raw, m)
-        quantize(p_codes[0], p_scales[0], p_bf[0][:])
-        for h in range(2):
-            product(0, h, p_codes, p_scales, k_codes, k_scales, True)
-        quantize_slots(u_codes, u_scales, u_bf, 0, "u_codes0", tag="p_bf0")
-        quantize(p_codes[1], p_scales[1], p_bf[1][:])
-        for h in range(2):
-            product(1, h, p_codes, p_scales, k_codes, k_scales, True)
+            lay_weights("scalar", q_bf, q_raw, m)
 
         def finish(m, h):
             product(m, h, q_codes, q_scales, u_codes, u_scales, False)
@@ -188,12 +185,17 @@ def tile_attend_pre_din_f_topk_kernel(tc, qT, pT, kT, rT, offs, offs2, out):
             nc.scalar.activation(res[:], acc[m, h][:], SIGMOID)
             nc.sync.dma_start(out[0, m * P : (m + 1) * P, h * HALF : (h + 1) * HALF], res[:])
 
-        quantize_slots(u_codes, u_scales, u_bf, 1, "u_codes1", tag="p_raw")
-        for m in range(2):
-            lay_weights("scalar", q_bf, q_raw, m)
+        quantize(p_codes[0], p_scales[0], p_bf[0][:])
+        for h in range(2):
+            product(0, h, p_codes, p_scales, k_codes, k_scales, True)
+        quantize_slots(u_codes, u_scales, u_bf, 0, "u_codes0", tag="p_raw0")
         quantize(q_codes[0], q_scales[0], q_bf[0][:])
         finish(0, 0)
+        quantize_slots(u_codes, u_scales, u_bf, 1, "u_codes1", tag="q_raw0")
         finish(0, 1)
+        quantize(p_codes[1], p_scales[1], p_bf[1][:])
+        for h in range(2):
+            product(1, h, p_codes, p_scales, k_codes, k_scales, True)
         quantize(q_codes[1], q_scales[1], q_bf[1][:])
         finish(1, 0)
         finish(1, 1)

@@ -23,8 +23,9 @@ HALF = SLOTS // 2
 QUARTER = SLOTS // 4
 LIST_COLS = SLOTS // 16
 DMA_ALIGN = 256
-FUSED = 96
-R3_CUTS = (FUSED, 160, 352, SLOTS)
+K3_CUTS = (0, 64, HALF, HALF + QUARTER, SLOTS)
+FUSED = 128
+R3_CUTS = (FUSED, 192, 352, SLOTS)
 
 FLOPS = 2 * 2 * D * NQ * SLOTS
 
@@ -155,12 +156,11 @@ def tile_attend_pre_din_f_topk_kernel(tc, qT, pT, kT, rT, offs, offs2, out):
         nc.vector.tensor_tensor(u_bf[:, :, 0:2], by_slot(r_first, 0, SLOTS), by_slot(k_pair[0], 0, SLOTS), MULT)
         gather_k("scalar", 2, 0, SLOTS)
 
-        gather_k("vector", 3, 0, QUARTER)
-        for c in range(1, 4):
-            gather_k("scalar", 3, c * QUARTER, (c + 1) * QUARTER)
-        lay_pair("vector", k_bf, k_pair[1], 1, 0, HALF)
-        lay_pair("vector", k_bf, k_pair[1], 1, HALF, HALF + QUARTER)
-        lay_pair("vector", k_bf, k_pair[1], 1, HALF + QUARTER, SLOTS)
+        k3_pieces = list(zip(K3_CUTS[:-1], K3_CUTS[1:]))
+        for c, (lo, hi) in enumerate(k3_pieces):
+            gather_k("vector" if c == 1 else "scalar", 3, lo, hi)
+        for lo, hi in k3_pieces:
+            lay_pair("vector", k_bf, k_pair[1], 1, lo, hi)
         for h in range(2):
             quantize_slots(k_codes, k_scales, k_bf, h, f"k_codes{h}")
 

@@ -26,6 +26,7 @@ DMA_ALIGN = 256
 K3_CUTS = (0, 64, HALF, HALF + QUARTER, SLOTS)
 FUSED = 128
 R3_CUTS = (FUSED, 192, 352, SLOTS)
+LAST = SLOTS - QUARTER
 
 FLOPS = 2 * 2 * D * NQ * SLOTS
 
@@ -121,11 +122,11 @@ def tile_attend_pre_din_f_topk_kernel(tc, qT, pT, kT, rT, offs, offs2, out):
                 u_bf[:, lo:hi, 2:4], by_slot(r_late, lo - FUSED, hi - FUSED), by_slot(k_pair[1], lo, hi), MULT
             )
 
-        def lay_weights(engine, dst, raw, m):
+        def lay_weights(engine, dst, raw, lo=0, hi=P):
             copy_on(
                 engine,
-                dst[m][:].rearrange("p (c i) t -> p c t i", i=4),
-                raw[m][:].rearrange("p t (c i) -> p c t i", i=4),
+                dst[:, lo:hi, :].rearrange("p (c i) t -> p c t i", i=4),
+                raw[:, :, lo:hi].rearrange("p t (c i) -> p c t i", i=4),
             )
 
         def quantize(codes, scales, src):
@@ -135,18 +136,28 @@ def tile_attend_pre_din_f_topk_kernel(tc, qT, pT, kT, rT, offs, offs2, out):
             codes[h] = mx_tile(name, [P, HALF], U32, tag=tag)
             quantize(codes[h], scales[h], src[:, h * HALF : (h + 1) * HALF, :])
 
-        acc = {(m, h): psum.tile([P, HALF], F32, name=f"acc{m}{h}") for m in range(2) for h in range(2)}
+        def bank(name, width, tag=None):
+            return psum.tile([P, width], F32, name=name, tag=tag or name)
 
-        def product(m, h, w_codes, w_scales, x_codes, x_scales, first):
+        def product(acc, m, lo, hi, w_codes, w_scales, x_codes, x_scales, first):
+            h = lo // HALF
+            cols = slice(lo - h * HALF, hi - h * HALF)
             nc.tensor.matmul_mx(
-                out=acc[m, h][:],
+                out=acc[:],
                 lhsT=w_codes[m][:].bitcast(FP8X4),
                 lhsT_scale=w_scales[m][:],
-                rhs=x_codes[h][:].bitcast(FP8X4),
-                rhs_scale=x_scales[h][:],
+                rhs=x_codes[h][:, cols].bitcast(FP8X4),
+                rhs_scale=x_scales[h][:, cols],
                 start=first,
                 stop=not first,
             )
+
+        def open_sum(acc, m, lo, hi):
+            product(acc, m, lo, hi, p_codes, p_scales, k_codes, k_scales, True)
+
+        def close_sum(acc, m, lo, hi, res):
+            product(acc, m, lo, hi, q_codes, q_scales, u_codes, u_scales, False)
+            nc.scalar.activation(res, acc[:], SIGMOID)
 
         gather_k("vector", 0, 0, SLOTS)
         gather_k("scalar", 1, 0, SLOTS)
@@ -175,27 +186,36 @@ def tile_attend_pre_din_f_topk_kernel(tc, qT, pT, kT, rT, offs, offs2, out):
         for lo, hi in pieces[1:]:
             multiply_and_lay(lo, hi)
 
-        for m in range(2):
-            lay_weights("scalar", p_bf, p_raw, m)
-            lay_weights("scalar", q_bf, q_raw, m)
+        lay_weights("scalar", p_bf[0], p_raw[0])
+        lay_weights("scalar", q_bf[0], q_raw[0])
+        lay_weights("scalar", p_bf[1], p_raw[1])
+        lay_weights("scalar", q_bf[1], q_raw[1])
 
-        def finish(m, h):
-            product(m, h, q_codes, q_scales, u_codes, u_scales, False)
-            res = sb.tile([P, HALF], F32, name=f"res{m}{h}", align_bytes=DMA_ALIGN)
-            nc.scalar.activation(res[:], acc[m, h][:], SIGMOID)
-            nc.sync.dma_start(out[0, m * P : (m + 1) * P, h * HALF : (h + 1) * HALF], res[:])
+        def result(name, width):
+            return sb.tile([P, width], F32, name=name, align_bytes=DMA_ALIGN)
 
+        top = [bank(f"top{h}", HALF) for h in range(2)]
+        top_res = result("top_res", SLOTS)
         quantize(p_codes[0], p_scales[0], p_bf[0][:])
         for h in range(2):
-            product(0, h, p_codes, p_scales, k_codes, k_scales, True)
+            open_sum(top[h], 0, h * HALF, (h + 1) * HALF)
         quantize_slots(u_codes, u_scales, u_bf, 0, "u_codes0", tag="p_raw0")
         quantize(q_codes[0], q_scales[0], q_bf[0][:])
-        finish(0, 0)
+        close_sum(top[0], 0, 0, HALF, top_res[:, :HALF])
         quantize_slots(u_codes, u_scales, u_bf, 1, "u_codes1", tag="q_raw0")
-        finish(0, 1)
+        close_sum(top[1], 0, HALF, SLOTS, top_res[:, HALF:])
+        nc.sync.dma_start(out[0, :P, :], top_res[:])
+
         quantize(p_codes[1], p_scales[1], p_bf[1][:])
-        for h in range(2):
-            product(1, h, p_codes, p_scales, k_codes, k_scales, True)
         quantize(q_codes[1], q_scales[1], q_bf[1][:])
-        finish(1, 0)
-        finish(1, 1)
+        for lo, hi in ((0, HALF), (HALF, LAST), (LAST, SLOTS)):
+            acc = bank(f"bottom{lo}", hi - lo)
+            res = result(f"bottom_res{lo}", hi - lo)
+            if lo == 0:
+                open_sum(acc, 1, lo, hi)
+                close_sum(acc, 1, lo, hi, res[:])
+            else:
+                product(acc, 1, lo, hi, q_codes, q_scales, u_codes, u_scales, True)
+                product(acc, 1, lo, hi, p_codes, p_scales, k_codes, k_scales, False)
+                nc.scalar.activation(res[:], acc[:], SIGMOID)
+            nc.sync.dma_start(out[0, P:, lo:hi], res[:])

@@ -27,6 +27,7 @@ K3_CUTS = (0, 64, HALF, HALF + QUARTER, SLOTS)
 FUSED = 128
 R3_CUTS = (FUSED, 192, 352, SLOTS)
 LAST = SLOTS - QUARTER
+Q1_CUT = 96
 
 FLOPS = 2 * 2 * D * NQ * SLOTS
 
@@ -189,7 +190,7 @@ def tile_attend_pre_din_f_topk_kernel(tc, qT, pT, kT, rT, offs, offs2, out):
         lay_weights("scalar", p_bf[0], p_raw[0])
         lay_weights("scalar", q_bf[0], q_raw[0])
         lay_weights("scalar", p_bf[1], p_raw[1])
-        lay_weights("scalar", q_bf[1], q_raw[1])
+        lay_weights("scalar", q_bf[1], q_raw[1], 0, Q1_CUT)
 
         def result(name, width):
             return sb.tile([P, width], F32, name=name, align_bytes=DMA_ALIGN)
@@ -207,6 +208,7 @@ def tile_attend_pre_din_f_topk_kernel(tc, qT, pT, kT, rT, offs, offs2, out):
         nc.sync.dma_start(out[0, :P, :], top_res[:])
 
         quantize(p_codes[1], p_scales[1], p_bf[1][:])
+        lay_weights("vector", q_bf[1], q_raw[1], Q1_CUT, P)
         quantize(q_codes[1], q_scales[1], q_bf[1][:])
         for lo, hi in ((0, HALF), (HALF, LAST), (LAST, SLOTS)):
             acc = bank(f"bottom{lo}", hi - lo)

from contextlib import ExitStack

import concourse.mybir as mybir

F32 = mybir.dt.float32
BF16 = mybir.dt.bfloat16
U32 = mybir.dt.uint32
U16 = mybir.dt.uint16
U8 = mybir.dt.uint8
FP8X4 = mybir.dt.float8_e4m3fn_x4
MULT = mybir.AluOpType.mult
SIGMOID = mybir.ActivationFunctionType.Sigmoid
COPY = mybir.ActivationFunctionType.Copy

P = 128
PACK = 4
D = 512
SLOTS = 512
NQ = 256
T_K = 2048
T_R = 1024
HALF = SLOTS // 2
QUARTER = SLOTS // 4
LIST_COLS = SLOTS // 16
DMA_ALIGN = 256
K3_CUTS = (0, 64, HALF, HALF + QUARTER, SLOTS)
FUSED = 128
R3_CUTS = (FUSED, 192, 352, SLOTS)
LAST = SLOTS - QUARTER
Q1_CUT = 96

FLOPS = 2 * 2 * D * NQ * SLOTS


def tile_attend_pre_din_f_topk_kernel(tc, qT, pT, kT, rT, offs, offs2, out):
    nc = tc.nc
    with ExitStack() as ctx:
        lists = ctx.enter_context(tc.tile_pool(name="lists", bufs=1))
        sb = ctx.enter_context(tc.tile_pool(name="sb", bufs=1))
        psum = ctx.enter_context(tc.psum_pool(name="psum", bufs=1))

        k_list = lists.tile([P, LIST_COLS], U16, name="k_list")
        r_list = lists.tile([P, LIST_COLS], U16, name="r_list")
        k_early = sb.tile([P, 2, T_K], F32, name="k_early", align_bytes=DMA_ALIGN)
        r_early = sb.tile([P, 2, T_R], F32, name="r_early", align_bytes=DMA_ALIGN)
        k_late = [sb.tile([P, T_K], F32, name=f"k_plane{t}", align_bytes=DMA_ALIGN) for t in (2, 3)]
        r_late_planes = [sb.tile([P, T_R], F32, name=f"r_plane{t}", align_bytes=DMA_ALIGN) for t in (2, 3)]
        k_plane = [k_early[:, 0, :], k_early[:, 1, :], k_late[0][:], k_late[1][:]]
        r_plane = [r_early[:, 0, :], r_early[:, 1, :], r_late_planes[0][:], r_late_planes[1][:]]
        p_raw = [sb.tile([P, PACK, P], F32, name=f"p_raw{m}", tag=f"p_raw{m}", align_bytes=DMA_ALIGN) for m in range(2)]
        q_raw = [sb.tile([P, PACK, P], F32, name=f"q_raw{m}", tag=f"q_raw{m}", align_bytes=DMA_ALIGN) for m in range(2)]

        k_rows = kT.rearrange("(p t) w -> p t w", t=PACK)
        r_rows = rT.rearrange("(p t) w -> p t w", t=PACK)

        nc.sync.dma_start(k_early[:], k_rows[:, 0:2, :])
        nc.sync.dma_start(k_list[:], offs)
        nc.sync.dma_start(r_list[:], offs2)
        nc.sync.dma_start(r_early[:], r_rows[:, 0:2, :])
        nc.sync.dma_start(k_plane[2], k_rows[:, 2, :])
        nc.sync.dma_start(k_plane[3], k_rows[:, 3, :])
        nc.sync.dma_start(r_plane[2], r_rows[:, 2, :])
        nc.sync.dma_start(r_plane[3], r_rows[:, 3, :])
        p_rows = pT[0].rearrange("(p t) w -> p t w", t=PACK)
        q_rows = qT[0].rearrange("(p t) w -> p t w", t=PACK)
        for m in range(2):
            nc.sync.dma_start(p_raw[m][:], p_rows[:, :, m * P : (m + 1) * P])
            nc.sync.dma_start(q_raw[m][:], q_rows[:, :, m * P : (m + 1) * P])

        warm_in = sb.tile([P, 1], F32, name="warm_in")
        warm_out = sb.tile([P, 1], F32, name="warm_out")
        nc.vector.memset(warm_in[:], 0.0)
        nc.scalar.activation(warm_out[:], warm_in[:], SIGMOID)

        k_pair = [sb.tile([P, 2, SLOTS], F32, name=f"k_pair{j}") for j in range(2)]
        r_first = sb.tile([P, 2, SLOTS], F32, name="r_first")
        u_late = sb.tile([P, 2, FUSED], F32, name="u_late")
        r_late = sb.tile([P, 2, SLOTS - FUSED], F32, name="r_late")

        def mx_tile(name, shape, dtype, tag=None):
            return sb.tile(shape, dtype, name=name, tag=tag or name, align_bytes=DMA_ALIGN)

        k_bf, u_bf = mx_tile("k_bf", [P, SLOTS, PACK], BF16), mx_tile("u_bf", [P, SLOTS, PACK], BF16)
        p_bf = [mx_tile(f"p_bf{m}", [P, P, PACK], BF16) for m in range(2)]
        q_bf = [mx_tile(f"q_bf{m}", [P, P, PACK], BF16) for m in range(2)]
        k_scales = [mx_tile(f"k_scales{h}", [P, HALF], U8) for h in range(2)]
        u_scales = [mx_tile(f"u_scales{h}", [P, HALF], U8) for h in range(2)]
        p_scales = [mx_tile(f"p_scales{m}", [P, P], U8) for m in range(2)]
        q_scales = [mx_tile(f"q_scales{m}", [P, P], U8) for m in range(2)]
        p_codes = [mx_tile(f"p_codes{m}", [P, P], U32) for m in range(2)]
        q_codes = [mx_tile(f"q_codes{m}", [P, P], U32) for m in range(2)]
        k_codes, u_codes = {}, {}

        def gather(engine, dst, plane, offsets, lo, hi):
            picked = plane.indirect(offsets[:, lo // 16 : hi // 16])
            if engine == "scalar":
                nc.scalar.activation(dst, picked, COPY)
            else:
                nc.vector.tensor_copy(dst, picked)

        def gather_k(engine, t, lo, hi):
            gather(engine, k_pair[t // 2][:, t % 2, lo:hi], k_plane[t], k_list, lo, hi)

        def gather_times_k(dst, t, hi):
            nc.vector.tensor_tensor(
                dst[:, t % 2, :], r_plane[t].indirect(r_list[:, : hi // 16]), k_pair[t // 2][:, t % 2, :hi], MULT
            )

        def copy_on(engine, dst, src):
            if engine == "scalar":
                nc.scalar.copy(dst, src)
            else:
                nc.vector.tensor_copy(dst, src)

        def by_slot(pair, lo, hi):
            return pair[:, :, lo:hi].rearrange("p e n -> p n e")

        def lay_pair(engine, dst, src, j, lo, hi):
            copy_on(engine, dst[:, lo:hi, 2 * j : 2 * j + 2], by_slot(src, lo, hi))

        def multiply_and_lay(lo, hi):
            nc.vector.tensor_tensor(
                u_bf[:, lo:hi, 2:4], by_slot(r_late, lo - FUSED, hi - FUSED), by_slot(k_pair[1], lo, hi), MULT
            )

        def lay_weights(engine, dst, raw, lo=0, hi=P):
            copy_on(
                engine,
                dst[:, lo:hi, :].rearrange("p (c i) t -> p c t i", i=4),
                raw[:, :, lo:hi].rearrange("p t (c i) -> p c t i", i=4),
            )

        def quantize(codes, scales, src):
            nc.vector.quantize_mx(out=codes[:].bitcast(FP8X4), scales=scales[:], in_=src.rearrange("p n t -> p (n t)"))

        def quantize_slots(codes, scales, src, h, name, tag=None):
            codes[h] = mx_tile(name, [P, HALF], U32, tag=tag)
            quantize(codes[h], scales[h], src[:, h * HALF : (h + 1) * HALF, :])

        def bank(name, width, tag=None):
            return psum.tile([P, width], F32, name=name, tag=tag or name)

        def product(acc, m, lo, hi, w_codes, w_scales, x_codes, x_scales, first):
            h = lo // HALF
            cols = slice(lo - h * HALF, hi - h * HALF)
            nc.tensor.matmul_mx(
                out=acc[:],
                lhsT=w_codes[m][:].bitcast(FP8X4),
                lhsT_scale=w_scales[m][:],
                rhs=x_codes[h][:, cols].bitcast(FP8X4),
                rhs_scale=x_scales[h][:, cols],
                start=first,
                stop=not first,
            )

        def open_sum(acc, m, lo, hi):
            product(acc, m, lo, hi, p_codes, p_scales, k_codes, k_scales, True)

        def close_sum(acc, m, lo, hi, res):
            product(acc, m, lo, hi, q_codes, q_scales, u_codes, u_scales, False)
            nc.scalar.activation(res, acc[:], SIGMOID)

        gather_k("vector", 0, 0, SLOTS)
        gather_k("scalar", 1, 0, SLOTS)
        lay_pair("vector", k_bf, k_pair[0], 0, 0, SLOTS)
        gather("vector", r_first[:, 0, :], r_plane[0], r_list, 0, SLOTS)
        gather("scalar", r_first[:, 1, :], r_plane[1], r_list, 0, SLOTS)
        nc.vector.tensor_tensor(u_bf[:, :, 0:2], by_slot(r_first, 0, SLOTS), by_slot(k_pair[0], 0, SLOTS), MULT)
        gather_k("scalar", 2, 0, SLOTS)

        k3_pieces = list(zip(K3_CUTS[:-1], K3_CUTS[1:]))
        for c, (lo, hi) in enumerate(k3_pieces):
            gather_k("vector" if c == 1 else "scalar", 3, lo, hi)
        for lo, hi in k3_pieces:
            lay_pair("vector", k_bf, k_pair[1], 1, lo, hi)
        for h in range(2):
            quantize_slots(k_codes, k_scales, k_bf, h, f"k_codes{h}")

        gather("scalar", r_late[:, 0, :], r_plane[2], r_list, FUSED, SLOTS)
        gather_times_k(u_late, 2, FUSED)
        gather_times_k(u_late, 3, FUSED)
        pieces = list(zip(R3_CUTS[:-1], R3_CUTS[1:]))
        for lo, hi in pieces:
            gather("scalar", r_late[:, 1, lo - FUSED : hi - FUSED], r_plane[3], r_list, lo, hi)
        multiply_and_lay(*pieces[0])
        lay_pair("vector", u_bf, u_late, 1, 0, FUSED)
        for lo, hi in pieces[1:]:
            multiply_and_lay(lo, hi)

        lay_weights("scalar", p_bf[0], p_raw[0])
        lay_weights("scalar", q_bf[0], q_raw[0])
        lay_weights("scalar", p_bf[1], p_raw[1])
        lay_weights("scalar", q_bf[1], q_raw[1], 0, Q1_CUT)

        def result(name, width):
            return sb.tile([P, width], F32, name=name, align_bytes=DMA_ALIGN)

        top = [bank(f"top{h}", HALF) for h in range(2)]
        top_res = result("top_res", SLOTS)
        quantize(p_codes[0], p_scales[0], p_bf[0][:])
        for h in range(2):
            open_sum(top[h], 0, h * HALF, (h + 1) * HALF)
        quantize_slots(u_codes, u_scales, u_bf, 0, "u_codes0", tag="p_raw0")
        quantize(q_codes[0], q_scales[0], q_bf[0][:])
        close_sum(top[0], 0, 0, HALF, top_res[:, :HALF])
        quantize_slots(u_codes, u_scales, u_bf, 1, "u_codes1", tag="q_raw0")
        close_sum(top[1], 0, HALF, SLOTS, top_res[:, HALF:])
        nc.sync.dma_start(out[0, :P, :], top_res[:])

        quantize(p_codes[1], p_scales[1], p_bf[1][:])
        lay_weights("vector", q_bf[1], q_raw[1], Q1_CUT, P)
        quantize(q_codes[1], q_scales[1], q_bf[1][:])
        for lo, hi in ((0, HALF), (HALF, LAST), (LAST, SLOTS)):
            acc = bank(f"bottom{lo}", hi - lo)
            res = result(f"bottom_res{lo}", hi - lo)
            if lo == 0:
                open_sum(acc, 1, lo, hi)
                close_sum(acc, 1, lo, hi, res[:])
            else:
                product(acc, 1, lo, hi, q_codes, q_scales, u_codes, u_scales, True)
                product(acc, 1, lo, hi, p_codes, p_scales, k_codes, k_scales, False)
                nc.scalar.activation(res[:], acc[:], SIGMOID)
            nc.sync.dma_start(out[0, P:, lo:hi], res[:])
